import numpy as np
import ml_dtypes


def mxq(x, axis, fmt="e4m3"):
    dtype, down = {"e4m3": (ml_dtypes.float8_e4m3fn, 7), "e5m2": (ml_dtypes.float8_e5m2, 14)}[fmt]
    v = np.moveaxis(np.asarray(x, np.float32).astype(ml_dtypes.bfloat16).astype(np.float64), axis, -1)
    blocks = v.reshape(v.shape[:-1] + (-1, 32))
    amax = np.abs(blocks).max(-1, keepdims=True)
    byte = np.maximum(np.where(amax > 0, np.frexp(amax)[1] - 1 + 127, 0) - down, 1)
    scale = np.exp2(byte - 127.0)
    codes = (blocks / scale).astype(np.float32).astype(dtype).astype(np.float64)
    return np.moveaxis((codes * scale).reshape(v.shape), -1, axis)


WIDE = False


def mx_kscale(k):
    if not WIDE:
        return np.ones(k)
    levels = np.array([30, -30])
    if k % 512:
        return np.exp2(np.random.permutation(np.resize(levels, k // 32))).repeat(32)
    a = np.empty((k // 512, 16))
    for p in range(k // 512):
        a[p, :8] = np.random.permutation(np.resize(levels, 8))
        for g in range(8):
            far = levels[np.abs(levels - a[p, g]) >= 10]
            a[p, g + 8] = far[np.random.randint(len(far))]
    return np.exp2(a.ravel()).repeat(32)


def f64(x):
    return np.asarray(x).astype(np.float64)


E2M1 = np.array([0.0, 0.5, 1.0, 1.5, 2.0, 3.0, 4.0, 6.0, -0.0, -0.5, -1.0, -1.5, -2.0, -3.0, -4.0, -6.0])


def pack_weight(w, fmt):
    k, n = w.shape
    w = f64(np.asarray(w, np.float32).astype(ml_dtypes.bfloat16)).reshape(k // 32, 32, n)
    amax = np.abs(w).max(1)
    if fmt == "e4m3":
        byte = np.frexp(amax)[1] - 1 + 127 - 7
    else:
        mant, ex = np.frexp(amax / 6.0)
        byte = np.where(mant > 0.5, ex, ex - 1) + 127
    byte = np.clip(np.where(amax > 0, byte, 1), 1, 254)
    scaled = (w * np.exp2(127.0 - byte)[:, None, :]).reshape(k, n).astype(np.float32)
    by_word = np.ascontiguousarray(scaled.reshape(k // 512, 128, 4, n).transpose(0, 1, 3, 2))
    if fmt == "e4m3":
        words = by_word.astype(ml_dtypes.float8_e4m3fn).view(np.uint8)
    else:
        c = by_word.astype(ml_dtypes.float4_e2m1fn).view(np.uint8) & 0xF
        words = (c[..., 0::2] | (c[..., 1::2] << 4)).reshape(k // 512, 128, 2 * n)
    return np.ascontiguousarray(words), np.ascontiguousarray(byte.astype(np.uint8).reshape(k // 512, 16, n))


def unpack_weight(words, scales, fmt):
    g, _, n = scales.shape
    words = np.ascontiguousarray(words).reshape(g, 128, n, -1)
    if fmt == "e4m3":
        vals = words.view(ml_dtypes.float8_e4m3fn).astype(np.float64)
    else:
        nib = np.empty((g, 128, n, 4), np.uint8)
        nib[..., 0::2] = words & 0xF
        nib[..., 1::2] = words >> 4
        vals = E2M1[nib]
    vals = vals * np.repeat(np.exp2(scales.astype(np.float64) - 127.0), 8, axis=1)[..., None]
    return vals.transpose(0, 1, 3, 2).reshape(g * 512, n)


def bf(x):
    return np.asarray(x, np.float32).astype(ml_dtypes.bfloat16)


def planes(Y):
    r, m = Y.shape
    b = f64(bf(Y)).reshape(r // 32, 32, m)
    amax = np.abs(b).max(1)
    byte = np.clip(np.where(amax > 0, np.frexp(amax)[1] - 1 + 127 - 7, 1), 1, 254)
    codes = (b * np.exp2(127.0 - byte)[:, None, :]).reshape(r, m).astype(np.float32).astype(ml_dtypes.float8_e4m3fn).view(np.uint8)
    words = codes.reshape(r // 512, 128, 4, m).transpose(0, 1, 3, 2)
    return np.ascontiguousarray(words), np.ascontiguousarray(byte.astype(np.uint8).reshape(r // 512, 16, m))


K, L, R, N, T = 512, 512, 512, 512, 512


def setup_inputs():
    n = np.random.standard_normal
    fk = mx_kscale(K)
    fr = mx_kscale(R)
    fl = mx_kscale(L)
    fn = mx_kscale(N)
    xtp = pack_weight(n((K, T)) / fk[:, None], "e2m1")
    wap = pack_weight(n((K, R)) * 1 / np.sqrt(K) * fk[:, None] * fr, "e4m3")
    xqp = pack_weight(n((L, T)) / fl[:, None], "e2m1")
    wcp = pack_weight(n((L, R)) * 1 / np.sqrt(L) * fl[:, None] * fr, "e4m3")
    wdp = pack_weight(n((N, R)) * 1 / np.sqrt(N) * fn[:, None], "e2m1")
    wup = pack_weight(n((R, K)) * 1 / np.sqrt(R) / fr[:, None], "e4m3")
    return {
        "xt_words": xtp[0],
        "xt_scales": xtp[1],
        "wa_words": wap[0],
        "wa_scales": wap[1],
        "xq_words": xqp[0],
        "xq_scales": xqp[1],
        "wc_words": wcp[0],
        "wc_scales": wcp[1],
        "g": (n((N, T)) * np.exp(0.5 * n((1, T))) / fn[:, None]).astype(np.float32),
        "wd_words": wdp[0],
        "wd_scales": wdp[1],
        "wu_words": wup[0],
        "wu_scales": wup[1],
    }


def reference(xt_words, xt_scales, wa_words, wa_scales, xq_words, xq_scales, wc_words, wc_scales, g, wd_words, wd_scales, wu_words, wu_scales):
    xtu = unpack_weight(xt_words, xt_scales, "e2m1")
    wau = unpack_weight(wa_words, wa_scales, "e4m3")
    xqu = unpack_weight(xq_words, xq_scales, "e2m1")
    wcu = unpack_weight(wc_words, wc_scales, "e4m3")
    wdu = unpack_weight(wd_words, wd_scales, "e2m1")
    wuu = unpack_weight(wu_words, wu_scales, "e4m3")
    z = wau.T @ xtu + wcu.T @ xqu
    gq = mxq(f64(g), 0, "e5m2")
    d = wdu.T @ gq
    dz = 2.0 * d * np.maximum(z, 0.0)
    dzq = mxq(dz, 0, "e5m2")
    y = wuu.T @ dzq
    words, scales = planes(y)
    return y, words, scales

@@ -1,0 +1,208 @@
+from contextlib import ExitStack
+
+import concourse.mybir as mybir
+from concourse.masks import make_identity
+
+F32 = mybir.dt.float32
+BF16 = mybir.dt.bfloat16
+I32 = mybir.dt.int32
+U32 = mybir.dt.uint32
+U8 = mybir.dt.uint8
+E4M3 = mybir.dt.float8_e4m3fn_x4
+E5M2 = mybir.dt.float8_e5m2_x4
+E2M1 = mybir.dt.float4_e2m1fn_x4
+ALU = mybir.AluOpType
+ACT = mybir.ActivationFunctionType
+
+P = 128
+W = 512
+CH = 128
+NCH = W // CH
+HALF = W // 2
+FLOPS = 4 * 2 * W * W * W
+
+
+def tile_mix_back_with_hidden_made_anew_pl_kernel(
+    tc, xt_words, xt_scales, wa_words, wa_scales, xq_words, xq_scales, wc_words, wc_scales,
+    g, wd_words, wd_scales, wu_words, wu_scales, out_0, out_1, out_2,
+):
+    nc = tc.nc
+    with ExitStack() as ctx:
+        keep = ctx.enter_context(tc.tile_pool(name="keep", bufs=1))
+        work = ctx.enter_context(tc.tile_pool(name="work", bufs=NCH))
+        psum = ctx.enter_context(tc.psum_pool(name="psum", bufs=NCH))
+        ctx.enter_context(tc.manual_schedule())
+
+        staged = [wd_scales, xt_scales, wa_scales, xq_scales, wc_scales]
+        stage = keep.tile([P, len(staged) * W], U8, align_bytes=64)
+        planes = keep.tile([P, len(staged) * W], U8, align_bytes=64)
+        wd_s, xt_s, wa_s, xq_s, wc_s = [planes[:, i * W:(i + 1) * W] for i in range(len(staged))]
+        xt = keep.tile([P, 2 * W], U8, align_bytes=64)
+        xq = keep.tile([P, 2 * W], U8, align_bytes=64)
+        wd = keep.tile([P, 2 * W], U8, align_bytes=64)
+        wa = keep.tile([P, W], U32, align_bytes=64)
+        wc = keep.tile([P, W], U32, align_bytes=64)
+        wu_raw = keep.tile([P, W], I32, align_bytes=64)
+        wu_s_raw = keep.tile([P, W], U8, align_bytes=64)
+        wu = keep.tile([P, W], I32, align_bytes=64)
+        wu_s = keep.tile([P, W], U8, align_bytes=64)
+        g_lo = keep.tile([P, 4, HALF], F32, align_bytes=64)
+        g_hi = keep.tile([P, 4, HALF], F32, align_bytes=64)
+        ident = keep.tile([P, P], F32, align_bytes=64)
+        warm = keep.tile([P, 8], F32, align_bytes=64)
+        dzq = keep.tile([P, W], U32, align_bytes=64)
+        dzq_s = keep.tile([P, W], U8, align_bytes=64)
+        y_sb = keep.tile([P, 4, W], F32, align_bytes=64)
+        y_codes = keep.tile([P, W], U32, align_bytes=64)
+        y_scales = keep.tile([P, W], U8, align_bytes=64)
+
+        def load4(queue, tile, words):
+            queue.dma_start(out=tile[:].bitcast(I32), in_=words[0].bitcast(I32))
+
+        def load8(queue, tile, words):
+            queue.dma_start(out=tile[:].bitcast(I32), in_=words[0].rearrange("p n t -> p (n t)").bitcast(I32))
+
+        g_rows = g.rearrange("(p j) t -> p j t", j=4)
+        y_rows = out_0.rearrange("(p j) t -> p j t", j=4)
+        code_rows = out_1[0].rearrange("p n t -> p (n t)").bitcast(I32)
+
+        for i, s in enumerate(staged):
+            queue = nc.sync if i % 2 else nc.scalar
+            queue.dma_start(out=stage[0:P:8, i * W:(i + 1) * W].bitcast(I32), in_=s[0].bitcast(I32))
+        load4(nc.sync, wd, wd_words)
+        nc.sync.dma_start(out=g_lo[:], in_=g_rows[:, :, 0:HALF])
+        nc.sync.dma_start(out=g_hi[:], in_=g_rows[:, :, HALF:W])
+        load8(nc.sync, wa, wa_words)
+        load8(nc.sync, wc, wc_words)
+        nc.vector.memset(warm[:], 0.0)
+        nc.vector.memset(planes[:].bitcast(U32), 0)
+        nc.scalar.activation(out=warm[:], in_=warm[:], func=ACT.Copy, scale=2.0)
+        for s in range(4):
+            nc.scalar.dma_start(out=planes[s:P:32, :].bitcast(I32), in_=stage[8 * s:P:32, :].bitcast(I32))
+        load4(nc.scalar, xt, xt_words)
+        load4(nc.scalar, xq, xq_words)
+        nc.gpsimd.memset(wu_s_raw[:].bitcast(U32), 0)
+        for q in range(4):
+            nc.gpsimd.dma_start(out=wu_s_raw[32 * q:32 * q + 4, :].bitcast(I32), in_=wu_scales[0, 4 * q:4 * q + 4, :].bitcast(I32))
+        make_identity(nc, ident[:])
+
+        g_bf, gq, gq_s, d_ps, z_ps, d2, dz_t, tr_ps, dz_bf, y_ps, y_bf = [{} for i in range(11)]
+
+        def interleave(copy, dst, src):
+            copy(out=dst.rearrange("p (c i) j -> p c j i", i=4), in_=src.rearrange("p j (c i) -> p c j i", i=4))
+
+        def cast_g(c):
+            g_bf[c] = work.tile([P, CH, 4], BF16, name="g_bf", align_bytes=64)
+            interleave(nc.vector.tensor_copy, g_bf[c][:], (g_lo, g_hi)[c // 2][:, :, (c % 2) * CH:(c % 2 + 1) * CH])
+
+        def quant_g(c):
+            gq[c] = work.tile([P, CH], U32, name="gq", align_bytes=64)
+            gq_s[c] = work.tile([P, CH], U8, name="gq_s", align_bytes=64)
+            nc.vector.quantize_mx(out=gq[c][:].bitcast(E5M2), scales=gq_s[c][:], in_=g_bf[c][:].rearrange("p t j -> p (t j)"))
+
+        def mm_d(c):
+            d_ps[c] = psum.tile([P, W], F32, name="first")
+            nc.tensor.matmul_mx(out=d_ps[c][:], lhsT=gq[c][:].bitcast(E5M2), lhsT_scale=gq_s[c][:],
+                                rhs=wd[:].bitcast(E2M1), rhs_scale=wd_s, start=True, stop=True)
+
+        def mm_z(c, i):
+            if i == 0:
+                z_ps[c] = psum.tile([P, W], F32, name="second")
+            x, xs, w, ws = ((xt, xt_s, wa, wa_s), (xq, xq_s, wc, wc_s))[i]
+            nc.tensor.matmul_mx(out=z_ps[c][:], lhsT=x[:, 2 * c * CH:2 * (c + 1) * CH].bitcast(E2M1),
+                                lhsT_scale=xs[:, c * CH:(c + 1) * CH], rhs=w[:].bitcast(E4M3), rhs_scale=ws,
+                                start=(i == 0), stop=(i == 1))
+
+        def drain_d(c):
+            d2[c] = work.tile([P, 2, P, 2], F32, name="d2", align_bytes=64)
+            nc.scalar.activation(out=d2[c][:], in_=d_ps[c][:].rearrange("t (p u e) -> t u p e", u=2, e=2), func=ACT.Copy, scale=2.0)
+
+        def mult(c):
+            dz_t[c] = work.tile([P, 2, P, 2], BF16, name="dz_t", align_bytes=64)
+            z = z_ps[c][:].rearrange("t (p u e) -> t u p e", u=2, e=2)
+            for u in range(2):
+                nc.vector.scalar_tensor_tensor(out=dz_t[c][:, u], in0=z[:, u], scalar=0.0, in1=d2[c][:, u], op0=ALU.max, op1=ALU.mult)
+
+        def turn_dz(c):
+            tr_ps[c] = psum.tile([P, W], F32, name="first")
+            words = dz_t[c][:].rearrange("t u p e -> t (u p e)").bitcast(F32)
+            for u in range(2):
+                nc.tensor.transpose(tr_ps[c][:, u * CH:(u + 1) * CH], words[:, u * P:(u + 1) * P], ident[:])
+
+        def copy_dz(c):
+            dz_bf[c] = work.tile([P, CH * 4], BF16, name="dz_bf", align_bytes=64)
+            nc.scalar.copy(out=dz_bf[c][:].bitcast(F32).rearrange("p (t u) -> p t u", u=2),
+                           in_=tr_ps[c][:, 0:2 * CH].rearrange("p (u t) -> p t u", u=2))
+
+        def quant_dz(c):
+            cols = slice(c * CH, (c + 1) * CH)
+            nc.vector.quantize_mx(out=dzq[:, cols].bitcast(E5M2), scales=dzq_s[:, cols], in_=dz_bf[c][:])
+
+        def mm_y(j):
+            cols = slice(j * P, (j + 1) * P)
+            y_ps[j] = psum.tile([P, W], F32, name="second")
+            nc.tensor.matmul_mx(out=y_ps[j][:], lhsT=wu[:, cols].bitcast(E4M3), lhsT_scale=wu_s[:, cols],
+                                rhs=dzq[:].bitcast(E5M2), rhs_scale=dzq_s[:], start=True, stop=True)
+
+        def drain_y(j):
+            copy = nc.vector.tensor_copy if j % 2 else nc.scalar.copy
+            for h in range(2):
+                cols = slice(h * HALF, (h + 1) * HALF)
+                copy(out=y_sb[:, j, cols], in_=y_ps[j][:, cols])
+            nc.sync.dma_start(out=y_rows[:, j, :], in_=y_sb[:, j, :])
+
+        def cast_y(c):
+            y_bf[c] = work.tile([P, CH, 4], BF16, name="y_bf", align_bytes=64)
+            copy = nc.vector.tensor_copy if c in (1, 2) else nc.scalar.copy
+            interleave(copy, y_bf[c][:], y_sb[:, :, c * CH:(c + 1) * CH])
+
+        def quant_y(c):
+            cols = slice(c * CH, (c + 1) * CH)
+            nc.vector.quantize_mx(out=y_codes[:, cols].bitcast(E4M3), scales=y_scales[:, cols], in_=y_bf[c][:].rearrange("p t j -> p (t j)"))
+
+        for pair in ((0, 1), (2, 3)):
+            for c in pair:
+                cast_g(c)
+            for c in pair:
+                quant_g(c)
+        mm_d(0)
+        mm_d(1)
+        drain_d(0)
+        load8(nc.scalar, wu_raw, wu_words)
+        drain_d(1)
+        mm_z(0, 0)
+        mm_d(2)
+        mm_d(3)
+        drain_d(2)
+        drain_d(3)
+        mm_z(1, 0)
+        mm_z(0, 1)
+        mm_z(1, 1)
+        for c in (2, 3):
+            mm_z(c, 0)
+            mm_z(c, 1)
+        for c in range(NCH):
+            mult(c)
+            turn_dz(c)
+            copy_dz(c)
+        nc.vector.tensor_copy(out=wu[:].rearrange("p (j c i) -> p c j i", j=4, i=4), in_=wu_raw[:].rearrange("p (c i j) -> p c j i", j=4, i=4))
+        quant_dz(0)
+        quant_dz(1)
+        nc.vector.tensor_copy(out=wu_s[:].rearrange("p (j c i) -> p c j i", j=4, i=16), in_=wu_s_raw[:].rearrange("p (c i j) -> p c j i", j=4, i=16))
+        quant_dz(2)
+        quant_dz(3)
+        for j in range(4):
+            mm_y(j)
+        for j in range(4):
+            drain_y(j)
+        for c in range(NCH):
+            cast_y(c)
+        for c in (1, 0):
+            quant_y(c)
+        nc.sync.dma_start(out=code_rows[:, 0:HALF], in_=y_codes[:, 0:HALF].bitcast(I32))
+        for c in (2, 3):
+            quant_y(c)
+        nc.sync.dma_start(out=code_rows[:, HALF:W], in_=y_codes[:, HALF:W].bitcast(I32))
+        for q in range(4):
+            queue = nc.sync if q % 2 else nc.scalar
+            queue.dma_start(out=out_2[0, 4 * q:4 * q + 4, :].bitcast(I32), in_=y_scales[32 * q:32 * q + 4, :].bitcast(I32))

@@ -71,8 +71,8 @@ def tile_mix_back_with_hidden_made_anew_pl_kernel(
             queue.dma_start(out=stage[0:P:8, i * W:(i + 1) * W].bitcast(I32), in_=s[0].bitcast(I32))
         load4(nc.sync, wd, wd_words)
         nc.sync.dma_start(out=g_lo[:], in_=g_rows[:, :, 0:HALF])
-        nc.sync.dma_start(out=g_hi[:], in_=g_rows[:, :, HALF:W])
         load8(nc.sync, wa, wa_words)
+        nc.sync.dma_start(out=g_hi[:], in_=g_rows[:, :, HALF:W])
         load8(nc.sync, wc, wc_words)
         nc.vector.memset(warm[:], 0.0)
         nc.vector.memset(planes[:].bitcast(U32), 0)
@@ -140,9 +140,12 @@ def tile_mix_back_with_hidden_made_anew_pl_kernel(
 
         def mm_y(j):
             cols = slice(j * P, (j + 1) * P)
-            y_ps[j] = psum.tile([P, W], F32, name="second")
             nc.tensor.matmul_mx(out=y_ps[j][:], lhsT=wu[:, cols].bitcast(E4M3), lhsT_scale=wu_s[:, cols],
                                 rhs=dzq[:].bitcast(E5M2), rhs_scale=dzq_s[:], start=True, stop=True)
+
+        def keep_warm(j):
+            nc.tensor.matmul_mx(out=y_ps[j][:], lhsT=xt[:, 0:2 * CH].bitcast(E2M1), lhsT_scale=xt_s[:, 0:CH],
+                                rhs=wa[:].bitcast(E4M3), rhs_scale=wa_s, start=True, stop=True)
 
         def drain_y(j):
             copy = nc.vector.tensor_copy if j % 2 else nc.scalar.copy
@@ -168,22 +171,24 @@ def tile_mix_back_with_hidden_made_anew_pl_kernel(
         mm_d(0)
         mm_d(1)
         drain_d(0)
-        load8(nc.scalar, wu_raw, wu_words)
         drain_d(1)
-        mm_z(0, 0)
+        load8(nc.scalar, wu_raw, wu_words)
+        for c in range(NCH):
+            mm_z(c, 0)
+        mm_z(0, 1)
+        mm_z(1, 1)
         mm_d(2)
         mm_d(3)
         drain_d(2)
         drain_d(3)
-        mm_z(1, 0)
-        mm_z(0, 1)
-        mm_z(1, 1)
-        for c in (2, 3):
-            mm_z(c, 0)
-            mm_z(c, 1)
+        mm_z(2, 1)
+        mm_z(3, 1)
         for c in range(NCH):
             mult(c)
+            y_ps[c] = psum.tile([P, W], F32, name="second")
             turn_dz(c)
+            for i in range((1, 1, 0, 3)[c]):
+                keep_warm(0)
             copy_dz(c)
         nc.vector.tensor_copy(out=wu[:].rearrange("p (j c i) -> p c j i", j=4, i=4), in_=wu_raw[:].rearrange("p (c i j) -> p c j i", j=4, i=4))
         quant_dz(0)

@@ -72,18 +72,20 @@ def tile_mix_back_with_hidden_made_anew_pl_kernel(
         load4(nc.sync, wd, wd_words)
         nc.sync.dma_start(out=g_lo[:], in_=g_rows[:, :, 0:HALF])
         load8(nc.sync, wa, wa_words)
-        nc.sync.dma_start(out=g_hi[:], in_=g_rows[:, :, HALF:W])
-        load8(nc.sync, wc, wc_words)
         nc.vector.memset(warm[:], 0.0)
         nc.vector.memset(planes[:].bitcast(U32), 0)
+        nc.vector.memset(wu_s_raw[:].bitcast(U32), 0)
         nc.scalar.activation(out=warm[:], in_=warm[:], func=ACT.Copy, scale=2.0)
         for s in range(4):
-            nc.scalar.dma_start(out=planes[s:P:32, :].bitcast(I32), in_=stage[8 * s:P:32, :].bitcast(I32))
+            queue = nc.sync if s % 2 else nc.scalar
+            queue.dma_start(out=planes[s:P:32, :].bitcast(I32), in_=stage[8 * s:P:32, :].bitcast(I32))
+        nc.sync.dma_start(out=g_hi[:], in_=g_rows[:, :, HALF:W])
+        load8(nc.sync, wc, wc_words)
         load4(nc.scalar, xt, xt_words)
         load4(nc.scalar, xq, xq_words)
-        nc.gpsimd.memset(wu_s_raw[:].bitcast(U32), 0)
+        load8(nc.sync, wu_raw, wu_words)
         for q in range(4):
-            nc.gpsimd.dma_start(out=wu_s_raw[32 * q:32 * q + 4, :].bitcast(I32), in_=wu_scales[0, 4 * q:4 * q + 4, :].bitcast(I32))
+            nc.sync.dma_start(out=wu_s_raw[32 * q:32 * q + 4, :].bitcast(I32), in_=wu_scales[0, 4 * q:4 * q + 4, :].bitcast(I32))
         make_identity(nc, ident[:])
 
         g_bf, gq, gq_s, d_ps, z_ps, d2, dz_t, tr_ps, dz_bf, y_ps, y_bf = [{} for i in range(11)]
@@ -152,7 +154,6 @@ def tile_mix_back_with_hidden_made_anew_pl_kernel(
             for h in range(2):
                 cols = slice(h * HALF, (h + 1) * HALF)
                 copy(out=y_sb[:, j, cols], in_=y_ps[j][:, cols])
-            nc.sync.dma_start(out=y_rows[:, j, :], in_=y_sb[:, j, :])
 
         def cast_y(c):
             y_bf[c] = work.tile([P, CH, 4], BF16, name="y_bf", align_bytes=64)
@@ -172,34 +173,33 @@ def tile_mix_back_with_hidden_made_anew_pl_kernel(
         mm_d(1)
         drain_d(0)
         drain_d(1)
-        load8(nc.scalar, wu_raw, wu_words)
-        for c in range(NCH):
-            mm_z(c, 0)
-        mm_z(0, 1)
-        mm_z(1, 1)
+        for i in range(2):
+            mm_z(0, i)
+            mm_z(1, i)
         mm_d(2)
         mm_d(3)
         drain_d(2)
         drain_d(3)
-        mm_z(2, 1)
-        mm_z(3, 1)
+        for c in (2, 3):
+            mm_z(c, 0)
+            mm_z(c, 1)
         for c in range(NCH):
             mult(c)
             y_ps[c] = psum.tile([P, W], F32, name="second")
             turn_dz(c)
-            for i in range((1, 1, 0, 3)[c]):
+            for i in range((0, 0, 0, 3)[c]):
                 keep_warm(0)
             copy_dz(c)
         nc.vector.tensor_copy(out=wu[:].rearrange("p (j c i) -> p c j i", j=4, i=4), in_=wu_raw[:].rearrange("p (c i j) -> p c j i", j=4, i=4))
-        quant_dz(0)
-        quant_dz(1)
         nc.vector.tensor_copy(out=wu_s[:].rearrange("p (j c i) -> p c j i", j=4, i=16), in_=wu_s_raw[:].rearrange("p (c i j) -> p c j i", j=4, i=16))
-        quant_dz(2)
-        quant_dz(3)
+        for c in range(NCH):
+            quant_dz(c)
         for j in range(4):
             mm_y(j)
-        for j in range(4):
-            drain_y(j)
+        for rows in ((0,), (1,), (2, 3)):
+            for j in rows:
+                drain_y(j)
+            nc.sync.dma_start(out=y_rows[:, rows[0]:rows[-1] + 1, :], in_=y_sb[:, rows[0]:rows[-1] + 1, :])
         for c in range(NCH):
             cast_y(c)
         for c in (1, 0):
@@ -207,7 +207,7 @@ def tile_mix_back_with_hidden_made_anew_pl_kernel(
         nc.sync.dma_start(out=code_rows[:, 0:HALF], in_=y_codes[:, 0:HALF].bitcast(I32))
         for c in (2, 3):
             quant_y(c)
-        nc.sync.dma_start(out=code_rows[:, HALF:W], in_=y_codes[:, HALF:W].bitcast(I32))
+        nc.scalar.dma_start(out=code_rows[:, HALF:W], in_=y_codes[:, HALF:W].bitcast(I32))
         for q in range(4):
-            queue = nc.sync if q % 2 else nc.scalar
+            queue = nc.scalar if q == 3 else nc.sync
             queue.dma_start(out=out_2[0, 4 * q:4 * q + 4, :].bitcast(I32), in_=y_scales[32 * q:32 * q + 4, :].bitcast(I32))

@@ -68,7 +68,7 @@ def tile_mix_back_with_hidden_made_anew_pl_kernel(
 
         for i, s in enumerate(staged):
             queue = nc.sync if i % 2 else nc.scalar
-            queue.dma_start(out=stage[0:P:8, i * W:(i + 1) * W].bitcast(I32), in_=s[0].bitcast(I32))
+            queue.dma_start(out=stage[4:P:8, i * W:(i + 1) * W].bitcast(I32), in_=s[0].bitcast(I32))
         load4(nc.sync, wd, wd_words)
         nc.sync.dma_start(out=g_lo[:], in_=g_rows[:, :, 0:HALF])
         load8(nc.sync, wa, wa_words)
@@ -78,7 +78,7 @@ def tile_mix_back_with_hidden_made_anew_pl_kernel(
         nc.scalar.activation(out=warm[:], in_=warm[:], func=ACT.Copy, scale=2.0)
         for s in range(4):
             queue = nc.sync if s % 2 else nc.scalar
-            queue.dma_start(out=planes[s:P:32, :].bitcast(I32), in_=stage[8 * s:P:32, :].bitcast(I32))
+            queue.dma_start(out=planes[s:P:32, :].bitcast(I32), in_=stage[4 + 8 * s:P:32, :].bitcast(I32))
         nc.sync.dma_start(out=g_hi[:], in_=g_rows[:, :, HALF:W])
         load8(nc.sync, wc, wc_words)
         load4(nc.scalar, xt, xt_words)
@@ -120,16 +120,16 @@ def tile_mix_back_with_hidden_made_anew_pl_kernel(
             nc.scalar.activation(out=d2[c][:], in_=d_ps[c][:].rearrange("t (p u e) -> t u p e", u=2, e=2), func=ACT.Copy, scale=2.0)
 
         def mult(c):
-            dz_t[c] = work.tile([P, 2, P, 2], BF16, name="dz_t", align_bytes=64)
             z = z_ps[c][:].rearrange("t (p u e) -> t u p e", u=2, e=2)
             for u in range(2):
-                nc.vector.scalar_tensor_tensor(out=dz_t[c][:, u], in0=z[:, u], scalar=0.0, in1=d2[c][:, u], op0=ALU.max, op1=ALU.mult)
+                dz_t[c, u] = work.tile([P, P, 2], BF16, name="dz_t", bufs=2 * NCH, align_bytes=64)
+                nc.vector.scalar_tensor_tensor(out=dz_t[c, u][:], in0=z[:, u], scalar=0.0, in1=d2[c][:, u], op0=ALU.max, op1=ALU.mult)
 
         def turn_dz(c):
             tr_ps[c] = psum.tile([P, W], F32, name="first")
-            words = dz_t[c][:].rearrange("t u p e -> t (u p e)").bitcast(F32)
             for u in range(2):
-                nc.tensor.transpose(tr_ps[c][:, u * CH:(u + 1) * CH], words[:, u * P:(u + 1) * P], ident[:])
+                words = dz_t[c, u][:].rearrange("t p e -> t (p e)").bitcast(F32)
+                nc.tensor.transpose(tr_ps[c][:, u * CH:(u + 1) * CH], words, ident[:])
 
         def copy_dz(c):
             dz_bf[c] = work.tile([P, CH * 4], BF16, name="dz_bf", align_bytes=64)
@@ -154,6 +154,8 @@ def tile_mix_back_with_hidden_made_anew_pl_kernel(
             for h in range(2):
                 cols = slice(h * HALF, (h + 1) * HALF)
                 copy(out=y_sb[:, j, cols], in_=y_ps[j][:, cols])
+                if j == 0:
+                    nc.sync.dma_start(out=y_rows[:, j, cols], in_=y_sb[:, j, cols])
 
         def cast_y(c):
             y_bf[c] = work.tile([P, CH, 4], BF16, name="y_bf", align_bytes=64)
@@ -183,6 +185,7 @@ def tile_mix_back_with_hidden_made_anew_pl_kernel(
         for c in (2, 3):
             mm_z(c, 0)
             mm_z(c, 1)
+        nc.gpsimd.tensor_copy(out=wu_s[:].rearrange("p (j c i) -> p c j i", j=4, i=16), in_=wu_s_raw[:].rearrange("p (c i j) -> p c j i", j=4, i=16))
         for c in range(NCH):
             mult(c)
             y_ps[c] = psum.tile([P, W], F32, name="second")
@@ -191,12 +194,12 @@ def tile_mix_back_with_hidden_made_anew_pl_kernel(
                 keep_warm(0)
             copy_dz(c)
         nc.vector.tensor_copy(out=wu[:].rearrange("p (j c i) -> p c j i", j=4, i=4), in_=wu_raw[:].rearrange("p (c i j) -> p c j i", j=4, i=4))
-        nc.vector.tensor_copy(out=wu_s[:].rearrange("p (j c i) -> p c j i", j=4, i=16), in_=wu_s_raw[:].rearrange("p (c i j) -> p c j i", j=4, i=16))
         for c in range(NCH):
             quant_dz(c)
         for j in range(4):
             mm_y(j)
-        for rows in ((0,), (1,), (2, 3)):
+        drain_y(0)
+        for rows in ((1,), (2, 3)):
             for j in rows:
                 drain_y(j)
             nc.sync.dma_start(out=y_rows[:, rows[0]:rows[-1] + 1, :], in_=y_sb[:, rows[0]:rows[-1] + 1, :])

from contextlib import ExitStack

import concourse.mybir as mybir
from concourse.masks import make_identity

F32 = mybir.dt.float32
BF16 = mybir.dt.bfloat16
I32 = mybir.dt.int32
U32 = mybir.dt.uint32
U8 = mybir.dt.uint8
E4M3 = mybir.dt.float8_e4m3fn_x4
E5M2 = mybir.dt.float8_e5m2_x4
E2M1 = mybir.dt.float4_e2m1fn_x4
ALU = mybir.AluOpType
ACT = mybir.ActivationFunctionType

P = 128
W = 512
CH = 128
NCH = W // CH
HALF = W // 2
FLOPS = 4 * 2 * W * W * W


def tile_mix_back_with_hidden_made_anew_pl_kernel(
    tc, xt_words, xt_scales, wa_words, wa_scales, xq_words, xq_scales, wc_words, wc_scales,
    g, wd_words, wd_scales, wu_words, wu_scales, out_0, out_1, out_2,
):
    nc = tc.nc
    with ExitStack() as ctx:
        keep = ctx.enter_context(tc.tile_pool(name="keep", bufs=1))
        work = ctx.enter_context(tc.tile_pool(name="work", bufs=NCH))
        psum = ctx.enter_context(tc.psum_pool(name="psum", bufs=NCH))
        ctx.enter_context(tc.manual_schedule())

        staged = [wd_scales, xt_scales, wa_scales, xq_scales, wc_scales]
        stage = keep.tile([P, len(staged) * W], U8, align_bytes=64)
        planes = keep.tile([P, len(staged) * W], U8, align_bytes=64)
        wd_s, xt_s, wa_s, xq_s, wc_s = [planes[:, i * W:(i + 1) * W] for i in range(len(staged))]
        xt = keep.tile([P, 2 * W], U8, align_bytes=64)
        xq = keep.tile([P, 2 * W], U8, align_bytes=64)
        wd = keep.tile([P, 2 * W], U8, align_bytes=64)
        wa = keep.tile([P, W], U32, align_bytes=64)
        wc = keep.tile([P, W], U32, align_bytes=64)
        wu_raw = keep.tile([P, W], I32, align_bytes=64)
        wu_s_raw = keep.tile([P, W], U8, align_bytes=64)
        wu = keep.tile([P, W], I32, align_bytes=64)
        wu_s = keep.tile([P, W], U8, align_bytes=64)
        g_lo = keep.tile([P, 4, HALF], F32, align_bytes=64)
        g_hi = keep.tile([P, 4, HALF], F32, align_bytes=64)
        ident = keep.tile([P, P], F32, align_bytes=64)
        warm = keep.tile([P, 8], F32, align_bytes=64)
        dzq = keep.tile([P, W], U32, align_bytes=64)
        dzq_s = keep.tile([P, W], U8, align_bytes=64)
        y_sb = keep.tile([P, 4, W], F32, align_bytes=64)
        y_codes = keep.tile([P, W], U32, align_bytes=64)
        y_scales = keep.tile([P, W], U8, align_bytes=64)

        def load4(queue, tile, words):
            queue.dma_start(out=tile[:].bitcast(I32), in_=words[0].bitcast(I32))

        def load8(queue, tile, words):
            queue.dma_start(out=tile[:].bitcast(I32), in_=words[0].rearrange("p n t -> p (n t)").bitcast(I32))

        g_rows = g.rearrange("(p j) t -> p j t", j=4)
        y_rows = out_0.rearrange("(p j) t -> p j t", j=4)
        code_rows = out_1[0].rearrange("p n t -> p (n t)").bitcast(I32)

        for i, s in enumerate(staged):
            queue = nc.sync if i % 2 else nc.scalar
            queue.dma_start(out=stage[4:P:8, i * W:(i + 1) * W].bitcast(I32), in_=s[0].bitcast(I32))
        load4(nc.sync, wd, wd_words)
        nc.sync.dma_start(out=g_lo[:], in_=g_rows[:, :, 0:HALF])
        load8(nc.sync, wa, wa_words)
        nc.vector.memset(warm[:], 0.0)
        nc.vector.memset(planes[:].bitcast(U32), 0)
        nc.vector.memset(wu_s_raw[:].bitcast(U32), 0)
        nc.scalar.activation(out=warm[:], in_=warm[:], func=ACT.Copy, scale=2.0)
        for s in range(4):
            queue = nc.sync if s % 2 else nc.scalar
            queue.dma_start(out=planes[s:P:32, :].bitcast(I32), in_=stage[4 + 8 * s:P:32, :].bitcast(I32))
        nc.sync.dma_start(out=g_hi[:], in_=g_rows[:, :, HALF:W])
        load8(nc.sync, wc, wc_words)
        load4(nc.scalar, xt, xt_words)
        load4(nc.scalar, xq, xq_words)
        load8(nc.sync, wu_raw, wu_words)
        for q in range(4):
            nc.sync.dma_start(out=wu_s_raw[32 * q:32 * q + 4, :].bitcast(I32), in_=wu_scales[0, 4 * q:4 * q + 4, :].bitcast(I32))
        make_identity(nc, ident[:])

        g_bf, gq, gq_s, d_ps, z_ps, d2, dz_t, tr_ps, dz_bf, y_ps, y_bf = [{} for i in range(11)]

        def interleave(copy, dst, src):
            copy(out=dst.rearrange("p (c i) j -> p c j i", i=4), in_=src.rearrange("p j (c i) -> p c j i", i=4))

        def cast_g(c):
            g_bf[c] = work.tile([P, CH, 4], BF16, name="g_bf", align_bytes=64)
            interleave(nc.vector.tensor_copy, g_bf[c][:], (g_lo, g_hi)[c // 2][:, :, (c % 2) * CH:(c % 2 + 1) * CH])

        def quant_g(c):
            gq[c] = work.tile([P, CH], U32, name="gq", align_bytes=64)
            gq_s[c] = work.tile([P, CH], U8, name="gq_s", align_bytes=64)
            nc.vector.quantize_mx(out=gq[c][:].bitcast(E5M2), scales=gq_s[c][:], in_=g_bf[c][:].rearrange("p t j -> p (t j)"))

        def mm_d(c):
            d_ps[c] = psum.tile([P, W], F32, name="first")
            nc.tensor.matmul_mx(out=d_ps[c][:], lhsT=gq[c][:].bitcast(E5M2), lhsT_scale=gq_s[c][:],
                                rhs=wd[:].bitcast(E2M1), rhs_scale=wd_s, start=True, stop=True)

        def mm_z(c, i):
            if i == 0:
                z_ps[c] = psum.tile([P, W], F32, name="second")
            x, xs, w, ws = ((xt, xt_s, wa, wa_s), (xq, xq_s, wc, wc_s))[i]
            nc.tensor.matmul_mx(out=z_ps[c][:], lhsT=x[:, 2 * c * CH:2 * (c + 1) * CH].bitcast(E2M1),
                                lhsT_scale=xs[:, c * CH:(c + 1) * CH], rhs=w[:].bitcast(E4M3), rhs_scale=ws,
                                start=(i == 0), stop=(i == 1))

        def drain_d(c):
            d2[c] = work.tile([P, 2, P, 2], F32, name="d2", align_bytes=64)
            nc.scalar.activation(out=d2[c][:], in_=d_ps[c][:].rearrange("t (p u e) -> t u p e", u=2, e=2), func=ACT.Copy, scale=2.0)

        def mult(c):
            z = z_ps[c][:].rearrange("t (p u e) -> t u p e", u=2, e=2)
            for u in range(2):
                dz_t[c, u] = work.tile([P, P, 2], BF16, name="dz_t", bufs=2 * NCH, align_bytes=64)
                nc.vector.scalar_tensor_tensor(out=dz_t[c, u][:], in0=z[:, u], scalar=0.0, in1=d2[c][:, u], op0=ALU.max, op1=ALU.mult)

        def turn_dz(c):
            tr_ps[c] = psum.tile([P, W], F32, name="first")
            for u in range(2):
                words = dz_t[c, u][:].rearrange("t p e -> t (p e)").bitcast(F32)
                nc.tensor.transpose(tr_ps[c][:, u * CH:(u + 1) * CH], words, ident[:])

        def copy_dz(c):
            dz_bf[c] = work.tile([P, CH * 4], BF16, name="dz_bf", align_bytes=64)
            nc.scalar.copy(out=dz_bf[c][:].bitcast(F32).rearrange("p (t u) -> p t u", u=2),
                           in_=tr_ps[c][:, 0:2 * CH].rearrange("p (u t) -> p t u", u=2))

        def quant_dz(c):
            cols = slice(c * CH, (c + 1) * CH)
            nc.vector.quantize_mx(out=dzq[:, cols].bitcast(E5M2), scales=dzq_s[:, cols], in_=dz_bf[c][:])

        def mm_y(j):
            cols = slice(j * P, (j + 1) * P)
            nc.tensor.matmul_mx(out=y_ps[j][:], lhsT=wu[:, cols].bitcast(E4M3), lhsT_scale=wu_s[:, cols],
                                rhs=dzq[:].bitcast(E5M2), rhs_scale=dzq_s[:], start=True, stop=True)

        def keep_warm(j):
            nc.tensor.matmul_mx(out=y_ps[j][:], lhsT=xt[:, 0:2 * CH].bitcast(E2M1), lhsT_scale=xt_s[:, 0:CH],
                                rhs=wa[:].bitcast(E4M3), rhs_scale=wa_s, start=True, stop=True)

        def drain_y(j):
            copy = nc.vector.tensor_copy if j % 2 else nc.scalar.copy
            for h in range(2):
                cols = slice(h * HALF, (h + 1) * HALF)
                copy(out=y_sb[:, j, cols], in_=y_ps[j][:, cols])
                if j == 0:
                    nc.sync.dma_start(out=y_rows[:, j, cols], in_=y_sb[:, j, cols])

        def cast_y(c):
            y_bf[c] = work.tile([P, CH, 4], BF16, name="y_bf", align_bytes=64)
            copy = nc.vector.tensor_copy if c in (1, 2) else nc.scalar.copy
            interleave(copy, y_bf[c][:], y_sb[:, :, c * CH:(c + 1) * CH])

        def quant_y(c):
            cols = slice(c * CH, (c + 1) * CH)
            nc.vector.quantize_mx(out=y_codes[:, cols].bitcast(E4M3), scales=y_scales[:, cols], in_=y_bf[c][:].rearrange("p t j -> p (t j)"))

        for pair in ((0, 1), (2, 3)):
            for c in pair:
                cast_g(c)
            for c in pair:
                quant_g(c)
        mm_d(0)
        mm_d(1)
        drain_d(0)
        drain_d(1)
        for i in range(2):
            mm_z(0, i)
            mm_z(1, i)
        mm_d(2)
        mm_d(3)
        drain_d(2)
        drain_d(3)
        for c in (2, 3):
            mm_z(c, 0)
            mm_z(c, 1)
        nc.gpsimd.tensor_copy(out=wu_s[:].rearrange("p (j c i) -> p c j i", j=4, i=16), in_=wu_s_raw[:].rearrange("p (c i j) -> p c j i", j=4, i=16))
        for c in range(NCH):
            mult(c)
            y_ps[c] = psum.tile([P, W], F32, name="second")
            turn_dz(c)
            for i in range((0, 0, 0, 3)[c]):
                keep_warm(0)
            copy_dz(c)
        nc.vector.tensor_copy(out=wu[:].rearrange("p (j c i) -> p c j i", j=4, i=4), in_=wu_raw[:].rearrange("p (c i j) -> p c j i", j=4, i=4))
        for c in range(NCH):
            quant_dz(c)
        for j in range(4):
            mm_y(j)
        drain_y(0)
        for rows in ((1,), (2, 3)):
            for j in rows:
                drain_y(j)
            nc.sync.dma_start(out=y_rows[:, rows[0]:rows[-1] + 1, :], in_=y_sb[:, rows[0]:rows[-1] + 1, :])
        for c in range(NCH):
            cast_y(c)
        for c in (1, 0):
            quant_y(c)
        nc.sync.dma_start(out=code_rows[:, 0:HALF], in_=y_codes[:, 0:HALF].bitcast(I32))
        for c in (2, 3):
            quant_y(c)
        nc.scalar.dma_start(out=code_rows[:, HALF:W], in_=y_codes[:, HALF:W].bitcast(I32))
        for q in range(4):
            queue = nc.scalar if q == 3 else nc.sync
            queue.dma_start(out=out_2[0, 4 * q:4 * q + 4, :].bitcast(I32), in_=y_scales[32 * q:32 * q + 4, :].bitcast(I32))
